import numpy as np, ml_dtypes
CORES = [36,164,52,180,100,228,116,244]
N = 8
TK = 32
def setup_inputs(rng):
    rt = (0.75 * rng.standard_normal((128, 1), dtype=np.float32) + rng.standard_normal((128, N), dtype=np.float32) / 2).astype(ml_dtypes.bfloat16)
    return {"x": rng.standard_normal((N, 128, TK), dtype=np.float32).astype(ml_dtypes.bfloat16), "rt": np.broadcast_to(rt, (N, 128, N)).copy(), "w": rng.standard_normal((N, 128, 128), dtype=np.float32).astype(ml_dtypes.bfloat16)}
def setup_inputs_big(rng):
    d = setup_inputs(rng)
    for k in ("x", "w"): d[k] = (d[k].astype(np.float32) * 1024.0).astype(d[k].dtype)
    return d
def setup_inputs_small(rng):
    d = setup_inputs(rng)
    for k in ("x", "w"): d[k] = (d[k].astype(np.float32) * (1 / 1024.0)).astype(d[k].dtype)
    return d
def reference(x, rt, w):
    X, RT, W = x.astype(np.float64), rt.astype(np.float64), w.astype(np.float64)
    y = np.zeros((N, 128, TK))
    for r in range(N):
        sc = RT[r].T @ X[r]
        g = np.exp(sc - sc.max(axis=0)); g = g / g.sum(axis=0)
        y[r] = sum(g[j] * (W[j].T @ X[r]) for j in range(N))
    return {"y": y.astype(ml_dtypes.bfloat16)}

@@ -1,0 +1,105 @@
+from concourse.bass import DstId, RemoteDMATransfer
+from concourse.mybir import AluOpType, AxisListType, ActivationFunctionType
+
+N = 8
+TK = 32
+D = 128
+
+SCRATCH = {
+    "wall": ("sbuf", [128, N * D], "bfloat16"),
+    "xs": ("sbuf", [128, TK], "bfloat16"),
+    "rts": ("sbuf", [128, N], "bfloat16"),
+    "ones": ("sbuf", [128, 128], "bfloat16"),
+    "ident": ("sbuf", [128, 128], "bfloat16"),
+    "negm": ("sbuf", [128, 4], "float32"),
+    "ex": ("sbuf", [128, N], "float32"),
+    "ssum": ("sbuf", [128, 4], "float32"),
+    "rs": ("sbuf", [128, 4], "float32"),
+    "xT": ("sbuf", [128, 128], "bfloat16"),
+    "dg": ("sbuf", [128, N * TK], "bfloat16"),
+    "xg": ("sbuf", [128, N * TK], "bfloat16"),
+    "ysb": ("sbuf", [128, TK], "bfloat16"),
+    "sc_ps": ("psum", [128, 512], "float32"),
+    "xT_ps": ("psum", [128, 1024], "bfloat16"),
+    "xg_ps": ("psum", [128, 512], "float32"),
+    "y_ps": ("psum", [128, 512], "float32"),
+}
+SEMAPHORES = ["s_w", "s_x", "s_ones", "s_id", "s_sc", "s_xT", "s_m", "s_e", "s_xTs", "s_r", "s_D", "s_xg", "s_xgs",
+              "s_y", "s_ys", "s_st", "sent"] + ["a%d" % j for j in range(N)]
+
+
+def rank_program(g, core, T, topo):
+    r = T.rank_of(core)
+    if r is None:
+        return
+    S = T.sem
+    cores = T.cores
+
+    def slot(j):
+        return T.wall[:, j * D:(j + 1) * D]
+
+    def tok(buf, j):
+        return buf[:, j * TK:(j + 1) * TK]
+
+    g.sync.dma_start(slot(r), T.w[:]).then_inc(S.s_w, 16)
+    g.scalar.dma_start(T.xs[:], T.x[:]).then_inc(S.s_x, 16)
+    g.scalar.dma_start(T.rts[:], T.rt[:]).then_inc(S.s_x, 16)
+
+    g.vector.memset(T.ones[:], 1.0).then_inc(S.s_ones, 1)
+    g.wait_ge(S.s_ones, 1)
+    g.affine_select(T.ident[:], T.ones[:], [[-1, 128]], AluOpType.is_equal, 0.0, 0, 1).then_inc(S.s_id, 1)
+
+    order = [(r + k) % N for k in range(1, N)]
+    mask = topo.mask(core, cores[order[0]])
+    ids = []
+    for j in order:
+        mask &= topo.mask(core, cores[j])
+        rid, pid = topo.addr(cores[j], core)
+        ids.append(DstId(rid=rid, pnc=pid))
+    neng = bin(mask).count("1")
+    g.wait_ge(S.s_w, 16)
+    g.remote_dma_fused([RemoteDMATransfer(dst_ids=ids, dma_engine_mask=mask, remote_sem=S["a%d" % r],
+                                          srcs=[slot(r)], dsts=[slot(r) for _ in order], alu_op=0)],
+                       local_sem=S.sent)
+
+    te, ve, ae = g.tensor, g.vector, g.scalar
+    te.wait_ge(S.s_x, 32)
+    te.matmul(T.sc_ps[0:TK, 0:N], T.xs[:], T.rts[:], True, True).then_inc(S.s_sc, 1)
+    te.wait_ge(S.s_id, 1)
+    te.transpose(T.xT_ps[0:TK, 0:128], T.xs[:], T.ident[:]).then_inc(S.s_xT, 1)
+
+    ve.wait_ge(S.s_sc, 1)
+    ve.tensor_reduce(T.negm[0:TK, 0:1], T.sc_ps[0:TK, 0:N], AxisListType.X, AluOpType.max, negate=True).then_inc(S.s_m, 1)
+    ae.wait_ge(S.s_m, 1)
+    ae.activation(T.ex[0:TK, 0:N], T.sc_ps[0:TK, 0:N], ActivationFunctionType.Exp, bias=T.negm[0:TK, 0:1], scale=1.0,
+                  accum_out=T.ssum[0:TK, 0:1]).then_inc(S.s_e, 1)
+    ve.wait_ge(S.s_xT, 1)
+    ve.tensor_copy(T.xT[0:TK, 0:128], T.xT_ps[0:TK, 0:128]).then_inc(S.s_xTs, 1)
+    ve.wait_ge(S.s_e, 1)
+    ve.reciprocal(T.rs[0:TK, 0:1], T.ssum[0:TK, 0:1]).then_inc(S.s_r, 1)
+    ve.wait_ge(S.s_r, 1)
+    ve.wait_ge(S.s_id, 1)
+    for j in range(N):
+        ve.tensor_scalar(T.dg[0:TK, j * TK:(j + 1) * TK], T.ident[0:TK, 0:TK], T.ex[0:TK, j:j + 1], T.rs[0:TK, 0:1],
+                         AluOpType.mult, AluOpType.mult).then_inc(S.s_D, 1)
+    te.wait_ge(S.s_D, N)
+    te.wait_ge(S.s_xTs, 1)
+    te.matmul(T.xg_ps[:, 0:N * TK], T.xT[0:TK, 0:128], T.dg[0:TK, 0:N * TK], True, True).then_inc(S.s_xg, 1)
+    ve.wait_ge(S.s_xg, 1)
+    ve.tensor_copy(T.xg[:], T.xg_ps[:, 0:N * TK]).then_inc(S.s_xgs, 1)
+
+    te.wait_ge(S.s_xgs, 1)
+    te.wait_ge(S.s_w, 16)
+    te.matmul(T.y_ps[:, 0:TK], slot(r), tok(T.xg, r), True, False)
+    for k in range(1, N):
+        j = (r - k) % N
+        te.wait_ge(S["a%d" % j], neng)
+        mm = te.matmul(T.y_ps[:, 0:TK], slot(j), tok(T.xg, j), False, k == N - 1)
+    mm.then_inc(S.s_y, 1)
+
+    ve.wait_ge(S.s_y, 1)
+    ve.tensor_copy(T.ysb[:], T.y_ps[:, 0:TK]).then_inc(S.s_ys, 1)
+    g.sync.wait_ge(S.s_ys, 1)
+    g.sync.dma_start(T.y[:], T.ysb[:]).then_inc(S.s_st, 16)
+    g.sync.wait_ge(S.s_st, 16)
+    g.wait_ge(S.sent, neng)

@@ -4,12 +4,15 @@ from concourse.mybir import AluOpType, AxisListType, ActivationFunctionType
 N = 8
 TK = 32
 D = 128
+HALF = D // 2
 
 SCRATCH = {
     "wall": ("sbuf", [128, N * D], "bfloat16"),
+    "wd": ("dram", [128, D], "bfloat16"),
     "xs": ("sbuf", [128, TK], "bfloat16"),
     "rts": ("sbuf", [128, N], "bfloat16"),
     "ones": ("sbuf", [128, 128], "bfloat16"),
+    "grid": ("sbuf", [128, 128], "bfloat16"),
     "ident": ("sbuf", [128, 128], "bfloat16"),
     "negm": ("sbuf", [128, 4], "float32"),
     "ex": ("sbuf", [128, N], "float32"),
@@ -17,37 +20,39 @@ SCRATCH = {
     "rs": ("sbuf", [128, 4], "float32"),
     "xT": ("sbuf", [128, 128], "bfloat16"),
     "dg": ("sbuf", [128, N * TK], "bfloat16"),
+    "dr": ("sbuf", [128, TK], "bfloat16"),
     "xg": ("sbuf", [128, N * TK], "bfloat16"),
+    "rsb": ("sbuf", [128, TK], "float32"),
     "ysb": ("sbuf", [128, TK], "bfloat16"),
     "sc_ps": ("psum", [128, 512], "float32"),
     "xT_ps": ("psum", [128, 1024], "bfloat16"),
-    "xg_ps": ("psum", [128, 512], "float32"),
+    "xgA_ps": ("psum", [128, 512], "float32"),
+    "xgB_ps": ("psum", [128, 512], "float32"),
+    "r_ps": ("psum", [128, 512], "float32"),
     "y_ps": ("psum", [128, 512], "float32"),
 }
-SEMAPHORES = ["s_w", "s_x", "s_ones", "s_id", "s_sc", "s_xT", "s_m", "s_e", "s_xTs", "s_r", "s_D", "s_xg", "s_xgs",
-              "s_y", "s_ys", "s_st", "sent"] + ["a%d" % j for j in range(N)]
+SEMAPHORES = ["s_wd", "s_w", "s_x", "s_ones", "s_gr", "s_grp", "s_id", "s_sc", "s_xT", "s_m", "s_e", "s_xTs", "s_r", "s_DA",
+              "s_DB", "s_dr", "s_xgA", "s_xgB", "s_xgsA", "s_xgsB", "s_R", "s_Rs", "s_y", "s_ys", "s_st", "sent"] \
+             + ["a%d" % j for j in range(N)]
+
+
+def _count(mask):
+    return bin(mask).count("1")
 
 
 def rank_program(g, core, T, topo):
+    cores = T.cores
     r = T.rank_of(core)
     if r is None:
         return
     S = T.sem
-    cores = T.cores
+    te, ve, ae = g.tensor, g.vector, g.scalar
 
     def slot(j):
         return T.wall[:, j * D:(j + 1) * D]
 
-    def tok(buf, j):
-        return buf[:, j * TK:(j + 1) * TK]
-
-    g.sync.dma_start(slot(r), T.w[:]).then_inc(S.s_w, 16)
-    g.scalar.dma_start(T.xs[:], T.x[:]).then_inc(S.s_x, 16)
-    g.scalar.dma_start(T.rts[:], T.rt[:]).then_inc(S.s_x, 16)
-
-    g.vector.memset(T.ones[:], 1.0).then_inc(S.s_ones, 1)
-    g.wait_ge(S.s_ones, 1)
-    g.affine_select(T.ident[:], T.ones[:], [[-1, 128]], AluOpType.is_equal, 0.0, 0, 1).then_inc(S.s_id, 1)
+    def blk(buf, p):
+        return buf[:, p * TK:(p + 1) * TK]
 
     order = [(r + k) % N for k in range(1, N)]
     mask = topo.mask(core, cores[order[0]])
@@ -56,13 +61,30 @@ def rank_program(g, core, T, topo):
         mask &= topo.mask(core, cores[j])
         rid, pid = topo.addr(cores[j], core)
         ids.append(DstId(rid=rid, pnc=pid))
-    neng = bin(mask).count("1")
-    g.wait_ge(S.s_w, 16)
+    neng = _count(mask)
+
+    g.sync.dma_start(T.wd[:], T.w[:]).then_inc(S.s_wd, 16)
+    g.scalar.dma_start(T.xs[:], T.x[:]).then_inc(S.s_x, 16)
+    g.scalar.dma_start(T.rts[:], T.rt[:]).then_inc(S.s_x, 16)
+    g.sync.dma_start(slot(r), T.w[:]).then_inc(S.s_w, 16)
+    ve.memset(T.ones[0:TK, 0:D], 1.0).then_inc(S.s_ones, 1)
+
+    h = r % 2
+    partner = cores[r + 1 - 2 * h]
+    mine = T.grid[:, h * HALF:(h + 1) * HALF]
+    g.iota(mine, [[-1, HALF]], -h * HALF, 1, allow_small_or_imprecise_dtypes=True).then_inc(S.s_gr, 1)
+    g.wait_ge(S.s_gr, 1)
+    rid, pid = topo.addr(partner, core)
+    g.remote_dma(mine, mine, S.s_grp, S.sent, pid, rid, mask)
+
+    g.wait_ge(S.s_wd, 16)
     g.remote_dma_fused([RemoteDMATransfer(dst_ids=ids, dma_engine_mask=mask, remote_sem=S["a%d" % r],
-                                          srcs=[slot(r)], dsts=[slot(r) for _ in order], alu_op=0)],
+                                          srcs=[T.wd[:]], dsts=[slot(r) for _ in order], alu_op=0)],
                        local_sem=S.sent)
 
-    te, ve, ae = g.tensor, g.vector, g.scalar
+    src = [(r - k) % N for k in range(N)]
+    H = N // 2
+
     te.wait_ge(S.s_x, 32)
     te.matmul(T.sc_ps[0:TK, 0:N], T.xs[:], T.rts[:], True, True).then_inc(S.s_sc, 1)
     te.wait_ge(S.s_id, 1)
@@ -73,33 +95,61 @@ def rank_program(g, core, T, topo):
     ae.wait_ge(S.s_m, 1)
     ae.activation(T.ex[0:TK, 0:N], T.sc_ps[0:TK, 0:N], ActivationFunctionType.Exp, bias=T.negm[0:TK, 0:1], scale=1.0,
                   accum_out=T.ssum[0:TK, 0:1]).then_inc(S.s_e, 1)
+    ve.wait_ge(S.s_gr, 1)
+    ve.wait_ge(S.s_grp, neng)
+    ve.tensor_scalar(T.ident[:], T.grid[:], 0.0, None, AluOpType.is_equal).then_inc(S.s_id, 1)
     ve.wait_ge(S.s_xT, 1)
     ve.tensor_copy(T.xT[0:TK, 0:128], T.xT_ps[0:TK, 0:128]).then_inc(S.s_xTs, 1)
-    ve.wait_ge(S.s_e, 1)
-    ve.reciprocal(T.rs[0:TK, 0:1], T.ssum[0:TK, 0:1]).then_inc(S.s_r, 1)
-    ve.wait_ge(S.s_r, 1)
-    ve.wait_ge(S.s_id, 1)
-    for j in range(N):
-        ve.tensor_scalar(T.dg[0:TK, j * TK:(j + 1) * TK], T.ident[0:TK, 0:TK], T.ex[0:TK, j:j + 1], T.rs[0:TK, 0:1],
-                         AluOpType.mult, AluOpType.mult).then_inc(S.s_D, 1)
-    te.wait_ge(S.s_D, N)
-    te.wait_ge(S.s_xTs, 1)
-    te.matmul(T.xg_ps[:, 0:N * TK], T.xT[0:TK, 0:128], T.dg[0:TK, 0:N * TK], True, True).then_inc(S.s_xg, 1)
-    ve.wait_ge(S.s_xg, 1)
-    ve.tensor_copy(T.xg[:], T.xg_ps[:, 0:N * TK]).then_inc(S.s_xgs, 1)
 
-    te.wait_ge(S.s_xgs, 1)
-    te.wait_ge(S.s_w, 16)
-    te.matmul(T.y_ps[:, 0:TK], slot(r), tok(T.xg, r), True, False)
-    for k in range(1, N):
-        j = (r - k) % N
-        te.wait_ge(S["a%d" % j], neng)
-        mm = te.matmul(T.y_ps[:, 0:TK], slot(j), tok(T.xg, j), False, k == N - 1)
+    ve.wait_ge(S.s_e, 1)
+    ve.wait_ge(S.s_id, 1)
+    for p in range(H):
+        j = src[p]
+        ve.tensor_scalar(T.dg[0:TK, p * TK:(p + 1) * TK], T.ident[0:TK, 0:TK], T.ex[0:TK, j:j + 1], None,
+                         AluOpType.mult).then_inc(S.s_DA, 1)
+    ae.wait_ge(S.s_e, 1)
+    ae.wait_ge(S.s_id, 1)
+    for p in range(H, N):
+        j = src[p]
+        ae.activation(T.dg[0:TK, p * TK:(p + 1) * TK], T.ident[0:TK, 0:TK], ActivationFunctionType.Identity,
+                      scale=T.ex[0:TK, j:j + 1]).then_inc(S.s_DB, 1)
+    ve.reciprocal(T.rs[0:TK, 0:1], T.ssum[0:TK, 0:1]).then_inc(S.s_r, 1)
+
+    te.wait_ge(S.s_xTs, 1)
+    te.wait_ge(S.s_DA, H)
+    te.matmul(T.xgA_ps[:, 0:H * TK], T.xT[0:TK, 0:128], T.dg[0:TK, 0:H * TK], True, True).then_inc(S.s_xgA, 1)
+    te.wait_ge(S.s_DB, H)
+    te.matmul(T.xgB_ps[:, 0:H * TK], T.xT[0:TK, 0:128], T.dg[0:TK, H * TK:N * TK], True, True).then_inc(S.s_xgB, 1)
+    ve.wait_ge(S.s_xgA, 1)
+    ve.tensor_copy(T.xg[:, 0:H * TK], T.xgA_ps[:, 0:H * TK]).then_inc(S.s_xgsA, 1)
+    ae.wait_ge(S.s_xgB, 1)
+    ae.activation(T.xg[:, H * TK:N * TK], T.xgB_ps[:, 0:H * TK], ActivationFunctionType.Identity).then_inc(S.s_xgsB, 1)
+
+    ve.wait_ge(S.s_r, 1)
+    ve.tensor_scalar(T.dr[0:TK, 0:TK], T.ident[0:TK, 0:TK], T.rs[0:TK, 0:1], None, AluOpType.mult).then_inc(S.s_dr, 1)
+
+    te.wait_ge(S.s_xgsA, 1)
+    for p in range(N):
+        j = src[p]
+        if p == N - 1:
+            te.wait_ge(S.s_dr, 1)
+            te.wait_ge(S.s_ones, 1)
+            te.matmul(T.r_ps[:, 0:TK], T.ones[0:TK, 0:D], T.dr[0:TK, 0:TK], True, True).then_inc(S.s_R, 1)
+        if p == 0:
+            te.wait_ge(S.s_w, 16)
+        else:
+            te.wait_ge(S["a%d" % j], neng)
+        if p == H:
+            te.wait_ge(S.s_xgsB, 1)
+        mm = te.matmul(T.y_ps[:, 0:TK], slot(j), blk(T.xg, p), p == 0, p == N - 1)
     mm.then_inc(S.s_y, 1)
 
+    ve.wait_ge(S.s_R, 1)
+    ve.tensor_copy(T.rsb[:], T.r_ps[:, 0:TK]).then_inc(S.s_Rs, 1)
+    ve.wait_ge(S.s_Rs, 1)
     ve.wait_ge(S.s_y, 1)
-    ve.tensor_copy(T.ysb[:], T.y_ps[:, 0:TK]).then_inc(S.s_ys, 1)
+    ve.tensor_tensor(T.ysb[:], T.y_ps[:, 0:TK], T.rsb[:], AluOpType.mult).then_inc(S.s_ys, 1)
     g.sync.wait_ge(S.s_ys, 1)
     g.sync.dma_start(T.y[:], T.ysb[:]).then_inc(S.s_st, 16)
     g.sync.wait_ge(S.s_st, 16)
-    g.wait_ge(S.sent, neng)
+    g.wait_ge(S.sent, 2 * neng)

@@ -4,35 +4,35 @@ from concourse.mybir import AluOpType, AxisListType, ActivationFunctionType
 N = 8
 TK = 32
 D = 128
-HALF = D // 2
+HALF = TK // 2
 
 SCRATCH = {
     "wall": ("sbuf", [128, N * D], "bfloat16"),
     "wd": ("dram", [128, D], "bfloat16"),
     "xs": ("sbuf", [128, TK], "bfloat16"),
+    "xrep": ("sbuf", [128, 4 * TK], "bfloat16"),
     "rts": ("sbuf", [128, N], "bfloat16"),
+    "zer": ("sbuf", [128, 128], "bfloat16"),
     "ones": ("sbuf", [128, 128], "bfloat16"),
-    "grid": ("sbuf", [128, 128], "bfloat16"),
-    "ident": ("sbuf", [128, 128], "bfloat16"),
+    "grid": ("sbuf", [128, TK], "bfloat16"),
+    "ident": ("sbuf", [128, TK], "bfloat16"),
     "negm": ("sbuf", [128, 4], "float32"),
     "ex": ("sbuf", [128, N], "float32"),
     "ssum": ("sbuf", [128, 4], "float32"),
     "rs": ("sbuf", [128, 4], "float32"),
-    "xT": ("sbuf", [128, 128], "bfloat16"),
     "dg": ("sbuf", [128, N * TK], "bfloat16"),
     "dr": ("sbuf", [128, TK], "bfloat16"),
     "xg": ("sbuf", [128, N * TK], "bfloat16"),
     "rsb": ("sbuf", [128, TK], "float32"),
     "ysb": ("sbuf", [128, TK], "bfloat16"),
     "sc_ps": ("psum", [128, 512], "float32"),
-    "xT_ps": ("psum", [128, 1024], "bfloat16"),
-    "xgA_ps": ("psum", [128, 512], "float32"),
-    "xgB_ps": ("psum", [128, 512], "float32"),
+    "gsA_ps": ("psum", [128, 512], "float32"),
+    "gsB_ps": ("psum", [128, 512], "float32"),
     "r_ps": ("psum", [128, 512], "float32"),
     "y_ps": ("psum", [128, 512], "float32"),
 }
-SEMAPHORES = ["s_wd", "s_w", "s_x", "s_ones", "s_gr", "s_grp", "s_id", "s_sc", "s_xT", "s_m", "s_e", "s_xTs", "s_r", "s_DA",
-              "s_DB", "s_dr", "s_xgA", "s_xgB", "s_xgsA", "s_xgsB", "s_R", "s_Rs", "s_y", "s_ys", "s_st", "sent"] \
+SEMAPHORES = ["s_wd", "s_w", "s_x", "s_z", "s_ones", "s_gr", "s_grp", "s_id", "s_sc", "s_xr", "s_m", "s_e", "s_r", "s_DA",
+              "s_DB", "s_dr", "s_gsA", "s_gsB", "s_xgsA", "s_xgsB", "s_R", "s_Rs", "s_y", "s_ys", "s_st", "sent"] \
              + ["a%d" % j for j in range(N)]
 
 
@@ -65,9 +65,12 @@ def rank_program(g, core, T, topo):
 
     g.sync.dma_start(T.wd[:], T.w[:]).then_inc(S.s_wd, 16)
     g.scalar.dma_start(T.xs[:], T.x[:]).then_inc(S.s_x, 16)
-    g.scalar.dma_start(T.rts[:], T.rt[:]).then_inc(S.s_x, 16)
+    g.sync.dma_start(T.rts[:], T.rt[:]).then_inc(S.s_x, 16)
     g.sync.dma_start(slot(r), T.w[:]).then_inc(S.s_w, 16)
-    ve.memset(T.ones[0:TK, 0:D], 1.0).then_inc(S.s_ones, 1)
+
+    ve.memset(T.zer[0:TK, 0:D], 0.0).then_inc(S.s_z, 1)
+    ae.wait_ge(S.s_z, 1)
+    ae.activation(T.ones[0:TK, 0:D], T.zer[0:TK, 0:D], ActivationFunctionType.Exp).then_inc(S.s_ones, 1)
 
     h = r % 2
     partner = cores[r + 1 - 2 * h]
@@ -87,26 +90,26 @@ def rank_program(g, core, T, topo):
 
     te.wait_ge(S.s_x, 32)
     te.matmul(T.sc_ps[0:TK, 0:N], T.xs[:], T.rts[:], True, True).then_inc(S.s_sc, 1)
-    te.wait_ge(S.s_id, 1)
-    te.transpose(T.xT_ps[0:TK, 0:128], T.xs[:], T.ident[:]).then_inc(S.s_xT, 1)
 
+    ve.wait_ge(S.s_x, 32)
+    for c in range(2):
+        ve.tensor_copy(blk(T.xrep, c), T.xs[:]).then_inc(S.s_xr, 1)
     ve.wait_ge(S.s_sc, 1)
     ve.tensor_reduce(T.negm[0:TK, 0:1], T.sc_ps[0:TK, 0:N], AxisListType.X, AluOpType.max, negate=True).then_inc(S.s_m, 1)
     ae.wait_ge(S.s_m, 1)
     ae.activation(T.ex[0:TK, 0:N], T.sc_ps[0:TK, 0:N], ActivationFunctionType.Exp, bias=T.negm[0:TK, 0:1], scale=1.0,
                   accum_out=T.ssum[0:TK, 0:1]).then_inc(S.s_e, 1)
+    for c in range(2, 4):
+        ve.tensor_copy(blk(T.xrep, c), T.xs[:]).then_inc(S.s_xr, 1)
     ve.wait_ge(S.s_gr, 1)
     ve.wait_ge(S.s_grp, neng)
-    ve.tensor_scalar(T.ident[:], T.grid[:], 0.0, None, AluOpType.is_equal).then_inc(S.s_id, 1)
-    ve.wait_ge(S.s_xT, 1)
-    ve.tensor_copy(T.xT[0:TK, 0:128], T.xT_ps[0:TK, 0:128]).then_inc(S.s_xTs, 1)
+    ve.tensor_scalar(T.ident[0:TK, 0:TK], T.grid[0:TK, 0:TK], 0.0, None, AluOpType.is_equal).then_inc(S.s_id, 1)
 
     ve.wait_ge(S.s_e, 1)
-    ve.wait_ge(S.s_id, 1)
     for p in range(H):
         j = src[p]
-        ve.tensor_scalar(T.dg[0:TK, p * TK:(p + 1) * TK], T.ident[0:TK, 0:TK], T.ex[0:TK, j:j + 1], None,
-                         AluOpType.mult).then_inc(S.s_DA, 1)
+        ve.tensor_scalar(T.dg[0:TK, p * TK:(p + 1) * TK], T.grid[0:TK, 0:TK], 0.0, T.ex[0:TK, j:j + 1],
+                         AluOpType.is_equal, AluOpType.mult).then_inc(S.s_DA, 1)
     ae.wait_ge(S.s_e, 1)
     ae.wait_ge(S.s_id, 1)
     for p in range(H, N):
@@ -115,25 +118,26 @@ def rank_program(g, core, T, topo):
                       scale=T.ex[0:TK, j:j + 1]).then_inc(S.s_DB, 1)
     ve.reciprocal(T.rs[0:TK, 0:1], T.ssum[0:TK, 0:1]).then_inc(S.s_r, 1)
 
-    te.wait_ge(S.s_xTs, 1)
+    te.wait_ge(S.s_ones, 1)
     te.wait_ge(S.s_DA, H)
-    te.matmul(T.xgA_ps[:, 0:H * TK], T.xT[0:TK, 0:128], T.dg[0:TK, 0:H * TK], True, True).then_inc(S.s_xgA, 1)
+    te.matmul(T.gsA_ps[:, 0:H * TK], T.ones[0:TK, 0:D], T.dg[0:TK, 0:H * TK], True, True).then_inc(S.s_gsA, 1)
     te.wait_ge(S.s_DB, H)
-    te.matmul(T.xgB_ps[:, 0:H * TK], T.xT[0:TK, 0:128], T.dg[0:TK, H * TK:N * TK], True, True).then_inc(S.s_xgB, 1)
-    ve.wait_ge(S.s_xgA, 1)
-    ve.tensor_copy(T.xg[:, 0:H * TK], T.xgA_ps[:, 0:H * TK]).then_inc(S.s_xgsA, 1)
-    ae.wait_ge(S.s_xgB, 1)
-    ae.activation(T.xg[:, H * TK:N * TK], T.xgB_ps[:, 0:H * TK], ActivationFunctionType.Identity).then_inc(S.s_xgsB, 1)
+    te.matmul(T.gsB_ps[:, 0:H * TK], T.ones[0:TK, 0:D], T.dg[0:TK, H * TK:N * TK], True, True).then_inc(S.s_gsB, 1)
+    ve.wait_ge(S.s_xr, 4)
+    ve.wait_ge(S.s_gsA, 1)
+    ve.tensor_tensor(T.xg[:, 0:H * TK], T.gsA_ps[:, 0:H * TK], T.xrep[:], AluOpType.mult).then_inc(S.s_xgsA, 1)
+    ve.wait_ge(S.s_gsB, 1)
+    ve.tensor_tensor(T.xg[:, H * TK:N * TK], T.gsB_ps[:, 0:H * TK], T.xrep[:], AluOpType.mult).then_inc(S.s_xgsB, 1)
 
     ve.wait_ge(S.s_r, 1)
-    ve.tensor_scalar(T.dr[0:TK, 0:TK], T.ident[0:TK, 0:TK], T.rs[0:TK, 0:1], None, AluOpType.mult).then_inc(S.s_dr, 1)
+    ve.tensor_scalar(T.dr[0:TK, 0:TK], T.grid[0:TK, 0:TK], 0.0, T.rs[0:TK, 0:1],
+                     AluOpType.is_equal, AluOpType.mult).then_inc(S.s_dr, 1)
 
     te.wait_ge(S.s_xgsA, 1)
     for p in range(N):
         j = src[p]
         if p == N - 1:
             te.wait_ge(S.s_dr, 1)
-            te.wait_ge(S.s_ones, 1)
             te.matmul(T.r_ps[:, 0:TK], T.ones[0:TK, 0:D], T.dr[0:TK, 0:TK], True, True).then_inc(S.s_R, 1)
         if p == 0:
             te.wait_ge(S.s_w, 16)

@@ -4,11 +4,12 @@ from concourse.mybir import AluOpType, AxisListType, ActivationFunctionType
 N = 8
 TK = 32
 D = 128
-HALF = TK // 2
+Q = TK // 4
 
 SCRATCH = {
     "wall": ("sbuf", [128, N * D], "bfloat16"),
     "wd": ("dram", [128, D], "bfloat16"),
+    "hl": ("dram", [128, D], "bfloat16"),
     "xs": ("sbuf", [128, TK], "bfloat16"),
     "xrep": ("sbuf", [128, 4 * TK], "bfloat16"),
     "rts": ("sbuf", [128, N], "bfloat16"),
@@ -31,8 +32,8 @@ SCRATCH = {
     "r_ps": ("psum", [128, 512], "float32"),
     "y_ps": ("psum", [128, 512], "float32"),
 }
-SEMAPHORES = ["s_wd", "s_w", "s_x", "s_z", "s_ones", "s_gr", "s_grp", "s_id", "s_sc", "s_xr", "s_m", "s_e", "s_r", "s_DA",
-              "s_DB", "s_dr", "s_gsA", "s_gsB", "s_xgsA", "s_xgsB", "s_R", "s_Rs", "s_y", "s_ys", "s_st", "sent"] \
+SEMAPHORES = ["s_wd", "s_w", "s_x", "s_z", "s_ones", "s_gr", "s_grp", "s_grh", "s_id", "s_sc", "s_xr", "s_m", "s_e", "s_r",
+              "s_DA", "s_DB", "s_dr", "s_gsA", "s_gsB", "s_xgsA", "s_xgsB", "s_R", "s_Rs", "s_y", "s_ys", "s_st", "sent"] \
              + ["a%d" % j for j in range(N)]
 
 
@@ -40,10 +41,47 @@ def _count(mask):
     return bin(mask).count("1")
 
 
+def _helper(topo, rc):
+    world = range(2 * topo.CORES_PER_HOST)
+    return [c for c in world if topo.host(c) == topo.host(rc) and topo.chip(c) == topo.chip(rc)
+            and topo.die(c) != topo.die(rc)][0]
+
+
+def _plan(topo, cores, r):
+    tos = [_helper(topo, cores[r])] + [cores[(r + k) % N] for k in range(1, N - 1)]
+    mask = topo.mask(cores[r], tos[0])
+    for to in tos:
+        mask &= topo.mask(cores[r], to)
+    return tos, mask
+
+
+def _helper_mask(topo, cores, d):
+    hc = _helper(topo, cores[d])
+    return topo.mask(hc, cores[d]) & topo.mask(hc, cores[(d - 1) % N])
+
+
+def _helper_program(g, core, T, topo, d):
+    S = T.sem
+    cores = T.cores
+    m = _helper_mask(topo, cores, d)
+    part = T.grid[:, 2 * Q:TK]
+    g.iota(part, [[-1, TK - 2 * Q]], -2 * Q, 1, allow_small_or_imprecise_dtypes=True).then_inc(S.s_gr, 1)
+    g.wait_ge(S.s_gr, 1)
+    rid, pid = topo.addr(cores[d], core)
+    g.remote_dma(part, part, S.s_grh, S.sent, pid, rid, m)
+    g.wait_ge(S["a%d" % d], _count(_plan(topo, cores, d)[1]))
+    rid, pid = topo.addr(cores[(d - 1) % N], core)
+    g.remote_dma(T.wall[:, d * D:(d + 1) * D], T.hl[:], S["a%d" % d], S.sent, pid, rid, m)
+    g.wait_ge(S.sent, 2 * _count(m))
+
+
 def rank_program(g, core, T, topo):
     cores = T.cores
     r = T.rank_of(core)
     if r is None:
+        for d in range(N):
+            if core == _helper(topo, cores[d]):
+                _helper_program(g, core, T, topo, d)
         return
     S = T.sem
     te, ve, ae = g.tensor, g.vector, g.scalar
@@ -54,13 +92,12 @@ def rank_program(g, core, T, topo):
     def blk(buf, p):
         return buf[:, p * TK:(p + 1) * TK]
 
-    order = [(r + k) % N for k in range(1, N)]
-    mask = topo.mask(core, cores[order[0]])
+    tos, mask = _plan(topo, cores, r)
     ids = []
-    for j in order:
-        mask &= topo.mask(core, cores[j])
-        rid, pid = topo.addr(cores[j], core)
+    for to in tos:
+        rid, pid = topo.addr(to, core)
         ids.append(DstId(rid=rid, pnc=pid))
+    dsts = [T.hl[:]] + [slot(r) for _ in tos[1:]]
     neng = _count(mask)
 
     g.sync.dma_start(T.wd[:], T.w[:]).then_inc(S.s_wd, 16)
@@ -74,18 +111,19 @@ def rank_program(g, core, T, topo):
 
     h = r % 2
     partner = cores[r + 1 - 2 * h]
-    mine = T.grid[:, h * HALF:(h + 1) * HALF]
-    g.iota(mine, [[-1, HALF]], -h * HALF, 1, allow_small_or_imprecise_dtypes=True).then_inc(S.s_gr, 1)
+    mine = T.grid[:, h * Q:(h + 1) * Q]
+    g.iota(mine, [[-1, Q]], -h * Q, 1, allow_small_or_imprecise_dtypes=True).then_inc(S.s_gr, 1)
     g.wait_ge(S.s_gr, 1)
     rid, pid = topo.addr(partner, core)
     g.remote_dma(mine, mine, S.s_grp, S.sent, pid, rid, mask)
 
     g.wait_ge(S.s_wd, 16)
     g.remote_dma_fused([RemoteDMATransfer(dst_ids=ids, dma_engine_mask=mask, remote_sem=S["a%d" % r],
-                                          srcs=[T.wd[:]], dsts=[slot(r) for _ in order], alu_op=0)],
+                                          srcs=[T.wd[:]], dsts=dsts, alu_op=0)],
                        local_sem=S.sent)
 
-    src = [(r - k) % N for k in range(N)]
+    korder = list(range(N - 2)) + [N - 1, N - 2]
+    src = [(r - k) % N for k in korder]
     H = N // 2
 
     te.wait_ge(S.s_x, 32)
@@ -103,6 +141,7 @@ def rank_program(g, core, T, topo):
         ve.tensor_copy(blk(T.xrep, c), T.xs[:]).then_inc(S.s_xr, 1)
     ve.wait_ge(S.s_gr, 1)
     ve.wait_ge(S.s_grp, neng)
+    ve.wait_ge(S.s_grh, _count(_helper_mask(topo, cores, r)))
     ve.tensor_scalar(T.ident[0:TK, 0:TK], T.grid[0:TK, 0:TK], 0.0, None, AluOpType.is_equal).then_inc(S.s_id, 1)
 
     ve.wait_ge(S.s_e, 1)
@@ -136,11 +175,13 @@ def rank_program(g, core, T, topo):
     te.wait_ge(S.s_xgsA, 1)
     for p in range(N):
         j = src[p]
-        if p == N - 1:
+        if p == N - 2:
             te.wait_ge(S.s_dr, 1)
             te.matmul(T.r_ps[:, 0:TK], T.ones[0:TK, 0:D], T.dr[0:TK, 0:TK], True, True).then_inc(S.s_R, 1)
         if p == 0:
             te.wait_ge(S.s_w, 16)
+        elif korder[p] == N - 1:
+            te.wait_ge(S["a%d" % j], _count(_helper_mask(topo, cores, j)))
         else:
             te.wait_ge(S["a%d" % j], neng)
         if p == H:

from concourse.bass import DstId, RemoteDMATransfer
from concourse.mybir import AluOpType, AxisListType, ActivationFunctionType

N = 8
TK = 32
D = 128
Q = TK // 4

SCRATCH = {
    "wall": ("sbuf", [128, N * D], "bfloat16"),
    "wd": ("dram", [128, D], "bfloat16"),
    "hl": ("dram", [128, D], "bfloat16"),
    "xs": ("sbuf", [128, TK], "bfloat16"),
    "xrep": ("sbuf", [128, 4 * TK], "bfloat16"),
    "rts": ("sbuf", [128, N], "bfloat16"),
    "zer": ("sbuf", [128, 128], "bfloat16"),
    "ones": ("sbuf", [128, 128], "bfloat16"),
    "grid": ("sbuf", [128, TK], "bfloat16"),
    "ident": ("sbuf", [128, TK], "bfloat16"),
    "negm": ("sbuf", [128, 4], "float32"),
    "ex": ("sbuf", [128, N], "float32"),
    "ssum": ("sbuf", [128, 4], "float32"),
    "rs": ("sbuf", [128, 4], "float32"),
    "dg": ("sbuf", [128, N * TK], "bfloat16"),
    "dr": ("sbuf", [128, TK], "bfloat16"),
    "xg": ("sbuf", [128, N * TK], "bfloat16"),
    "rsb": ("sbuf", [128, TK], "float32"),
    "ysb": ("sbuf", [128, TK], "bfloat16"),
    "sc_ps": ("psum", [128, 512], "float32"),
    "gsA_ps": ("psum", [128, 512], "float32"),
    "gsB_ps": ("psum", [128, 512], "float32"),
    "r_ps": ("psum", [128, 512], "float32"),
    "y_ps": ("psum", [128, 512], "float32"),
}
SEMAPHORES = ["s_wd", "s_w", "s_x", "s_z", "s_ones", "s_gr", "s_grp", "s_grh", "s_id", "s_sc", "s_xr", "s_m", "s_e", "s_r",
              "s_DA", "s_DB", "s_dr", "s_gsA", "s_gsB", "s_xgsA", "s_xgsB", "s_R", "s_Rs", "s_y", "s_ys", "s_st", "sent"] \
             + ["a%d" % j for j in range(N)]


def _count(mask):
    return bin(mask).count("1")


def _helper(topo, rc):
    world = range(2 * topo.CORES_PER_HOST)
    return [c for c in world if topo.host(c) == topo.host(rc) and topo.chip(c) == topo.chip(rc)
            and topo.die(c) != topo.die(rc)][0]


def _plan(topo, cores, r):
    tos = [_helper(topo, cores[r])] + [cores[(r + k) % N] for k in range(1, N - 1)]
    mask = topo.mask(cores[r], tos[0])
    for to in tos:
        mask &= topo.mask(cores[r], to)
    return tos, mask


def _helper_mask(topo, cores, d):
    hc = _helper(topo, cores[d])
    return topo.mask(hc, cores[d]) & topo.mask(hc, cores[(d - 1) % N])


def _helper_program(g, core, T, topo, d):
    S = T.sem
    cores = T.cores
    m = _helper_mask(topo, cores, d)
    part = T.grid[:, 2 * Q:TK]
    g.iota(part, [[-1, TK - 2 * Q]], -2 * Q, 1, allow_small_or_imprecise_dtypes=True).then_inc(S.s_gr, 1)
    g.wait_ge(S.s_gr, 1)
    rid, pid = topo.addr(cores[d], core)
    g.remote_dma(part, part, S.s_grh, S.sent, pid, rid, m)
    g.wait_ge(S["a%d" % d], _count(_plan(topo, cores, d)[1]))
    rid, pid = topo.addr(cores[(d - 1) % N], core)
    g.remote_dma(T.wall[:, d * D:(d + 1) * D], T.hl[:], S["a%d" % d], S.sent, pid, rid, m)
    g.wait_ge(S.sent, 2 * _count(m))


def rank_program(g, core, T, topo):
    cores = T.cores
    r = T.rank_of(core)
    if r is None:
        for d in range(N):
            if core == _helper(topo, cores[d]):
                _helper_program(g, core, T, topo, d)
        return
    S = T.sem
    te, ve, ae = g.tensor, g.vector, g.scalar

    def slot(j):
        return T.wall[:, j * D:(j + 1) * D]

    def blk(buf, p):
        return buf[:, p * TK:(p + 1) * TK]

    tos, mask = _plan(topo, cores, r)
    ids = []
    for to in tos:
        rid, pid = topo.addr(to, core)
        ids.append(DstId(rid=rid, pnc=pid))
    dsts = [T.hl[:]] + [slot(r) for _ in tos[1:]]
    neng = _count(mask)

    g.sync.dma_start(T.wd[:], T.w[:]).then_inc(S.s_wd, 16)
    g.scalar.dma_start(T.xs[:], T.x[:]).then_inc(S.s_x, 16)
    g.sync.dma_start(T.rts[:], T.rt[:]).then_inc(S.s_x, 16)
    g.sync.dma_start(slot(r), T.w[:]).then_inc(S.s_w, 16)

    ve.memset(T.zer[0:TK, 0:D], 0.0).then_inc(S.s_z, 1)
    ae.wait_ge(S.s_z, 1)
    ae.activation(T.ones[0:TK, 0:D], T.zer[0:TK, 0:D], ActivationFunctionType.Exp).then_inc(S.s_ones, 1)

    h = r % 2
    partner = cores[r + 1 - 2 * h]
    mine = T.grid[:, h * Q:(h + 1) * Q]
    g.iota(mine, [[-1, Q]], -h * Q, 1, allow_small_or_imprecise_dtypes=True).then_inc(S.s_gr, 1)
    g.wait_ge(S.s_gr, 1)
    rid, pid = topo.addr(partner, core)
    g.remote_dma(mine, mine, S.s_grp, S.sent, pid, rid, mask)

    g.wait_ge(S.s_wd, 16)
    g.remote_dma_fused([RemoteDMATransfer(dst_ids=ids, dma_engine_mask=mask, remote_sem=S["a%d" % r],
                                          srcs=[T.wd[:]], dsts=dsts, alu_op=0)],
                       local_sem=S.sent)

    korder = list(range(N - 2)) + [N - 1, N - 2]
    src = [(r - k) % N for k in korder]
    H = N // 2

    te.wait_ge(S.s_x, 32)
    te.matmul(T.sc_ps[0:TK, 0:N], T.xs[:], T.rts[:], True, True).then_inc(S.s_sc, 1)

    ve.wait_ge(S.s_x, 32)
    for c in range(2):
        ve.tensor_copy(blk(T.xrep, c), T.xs[:]).then_inc(S.s_xr, 1)
    ve.wait_ge(S.s_sc, 1)
    ve.tensor_reduce(T.negm[0:TK, 0:1], T.sc_ps[0:TK, 0:N], AxisListType.X, AluOpType.max, negate=True).then_inc(S.s_m, 1)
    ae.wait_ge(S.s_m, 1)
    ae.activation(T.ex[0:TK, 0:N], T.sc_ps[0:TK, 0:N], ActivationFunctionType.Exp, bias=T.negm[0:TK, 0:1], scale=1.0,
                  accum_out=T.ssum[0:TK, 0:1]).then_inc(S.s_e, 1)
    for c in range(2, 4):
        ve.tensor_copy(blk(T.xrep, c), T.xs[:]).then_inc(S.s_xr, 1)
    ve.wait_ge(S.s_gr, 1)
    ve.wait_ge(S.s_grp, neng)
    ve.wait_ge(S.s_grh, _count(_helper_mask(topo, cores, r)))
    ve.tensor_scalar(T.ident[0:TK, 0:TK], T.grid[0:TK, 0:TK], 0.0, None, AluOpType.is_equal).then_inc(S.s_id, 1)

    ve.wait_ge(S.s_e, 1)
    for p in range(H):
        j = src[p]
        ve.tensor_scalar(T.dg[0:TK, p * TK:(p + 1) * TK], T.grid[0:TK, 0:TK], 0.0, T.ex[0:TK, j:j + 1],
                         AluOpType.is_equal, AluOpType.mult).then_inc(S.s_DA, 1)
    ae.wait_ge(S.s_e, 1)
    ae.wait_ge(S.s_id, 1)
    for p in range(H, N):
        j = src[p]
        ae.activation(T.dg[0:TK, p * TK:(p + 1) * TK], T.ident[0:TK, 0:TK], ActivationFunctionType.Identity,
                      scale=T.ex[0:TK, j:j + 1]).then_inc(S.s_DB, 1)
    ve.reciprocal(T.rs[0:TK, 0:1], T.ssum[0:TK, 0:1]).then_inc(S.s_r, 1)

    te.wait_ge(S.s_ones, 1)
    te.wait_ge(S.s_DA, H)
    te.matmul(T.gsA_ps[:, 0:H * TK], T.ones[0:TK, 0:D], T.dg[0:TK, 0:H * TK], True, True).then_inc(S.s_gsA, 1)
    te.wait_ge(S.s_DB, H)
    te.matmul(T.gsB_ps[:, 0:H * TK], T.ones[0:TK, 0:D], T.dg[0:TK, H * TK:N * TK], True, True).then_inc(S.s_gsB, 1)
    ve.wait_ge(S.s_xr, 4)
    ve.wait_ge(S.s_gsA, 1)
    ve.tensor_tensor(T.xg[:, 0:H * TK], T.gsA_ps[:, 0:H * TK], T.xrep[:], AluOpType.mult).then_inc(S.s_xgsA, 1)
    ve.wait_ge(S.s_gsB, 1)
    ve.tensor_tensor(T.xg[:, H * TK:N * TK], T.gsB_ps[:, 0:H * TK], T.xrep[:], AluOpType.mult).then_inc(S.s_xgsB, 1)

    ve.wait_ge(S.s_r, 1)
    ve.tensor_scalar(T.dr[0:TK, 0:TK], T.grid[0:TK, 0:TK], 0.0, T.rs[0:TK, 0:1],
                     AluOpType.is_equal, AluOpType.mult).then_inc(S.s_dr, 1)

    te.wait_ge(S.s_xgsA, 1)
    for p in range(N):
        j = src[p]
        if p == N - 2:
            te.wait_ge(S.s_dr, 1)
            te.matmul(T.r_ps[:, 0:TK], T.ones[0:TK, 0:D], T.dr[0:TK, 0:TK], True, True).then_inc(S.s_R, 1)
        if p == 0:
            te.wait_ge(S.s_w, 16)
        elif korder[p] == N - 1:
            te.wait_ge(S["a%d" % j], _count(_helper_mask(topo, cores, j)))
        else:
            te.wait_ge(S["a%d" % j], neng)
        if p == H:
            te.wait_ge(S.s_xgsB, 1)
        mm = te.matmul(T.y_ps[:, 0:TK], slot(j), blk(T.xg, p), p == 0, p == N - 1)
    mm.then_inc(S.s_y, 1)

    ve.wait_ge(S.s_R, 1)
    ve.tensor_copy(T.rsb[:], T.r_ps[:, 0:TK]).then_inc(S.s_Rs, 1)
    ve.wait_ge(S.s_Rs, 1)
    ve.wait_ge(S.s_y, 1)
    ve.tensor_tensor(T.ysb[:], T.y_ps[:, 0:TK], T.rsb[:], AluOpType.mult).then_inc(S.s_ys, 1)
    g.sync.wait_ge(S.s_ys, 1)
    g.sync.dma_start(T.y[:], T.ysb[:]).then_inc(S.s_st, 16)
    g.sync.wait_ge(S.s_st, 16)
    g.wait_ge(S.sent, 2 * neng)
